import numpy as np, ml_dtypes
CORES = [2,10,18,26,34,42,50,58]
N = 8
def setup_inputs(rng):
    return {"x": rng.standard_normal((N, 128, 4), dtype=np.float32).astype(ml_dtypes.bfloat16)}
def reference(x):
    g = np.concatenate(list(x), axis=1)
    return {"y": np.broadcast_to(g, (N,) + g.shape)}

@@ -1,0 +1,32 @@
+from concourse.bass import DstId, RemoteDMATransfer
+
+SCRATCH = {
+    "land": ("sbuf", [128, 32], "bfloat16"),
+}
+SEMAPHORES = ["loaded", "arrived", "stored"]
+
+W = 4
+
+
+def rank_program(g, core, T, topo):
+    rank = T.rank_of(core)
+    if rank is None:
+        return
+    peers = [c for c in T.cores if c != core]
+    mine = T.land[:, W * rank:W * (rank + 1)]
+
+    g.dma_start(mine, T.x[:, :]).then_inc(T.sem.loaded, 16)
+    g.wait_ge(T.sem.loaded, 16)
+
+    ids = []
+    for p in peers:
+        rid, pid, _se = topo.addr(p)
+        ids.append(DstId(rid=rid, pnc=pid))
+    g.remote_dma_fused(
+        [RemoteDMATransfer(dst_ids=ids, dma_engine_mask=0x00FF, remote_sem=T.sem.arrived,
+                           srcs=[mine], dsts=[mine] * len(peers))],
+        local_sem=T.sem.arrived)
+
+    g.wait_ge(T.sem.arrived, 8 * len(peers) + 8)
+    g.dma_start(T.y[:, :], T.land[:, :]).then_inc(T.sem.stored, 16)
+    g.wait_ge(T.sem.stored, 16)

@@ -12,7 +12,15 @@ def rank_program(g, core, T, topo):
     rank = T.rank_of(core)
     if rank is None:
         return
-    peers = [c for c in T.cores if c != core]
+    me = topo.chip(core)
+
+    def way(c):
+        other = topo.chip(c)
+        if topo.mates(me, other):
+            return 0
+        return 1 if topo.same_plane(me, other) else 2
+
+    peers = sorted((c for c in T.cores if c != core), key=way, reverse=True)
     mine = T.land[:, W * rank:W * (rank + 1)]
 
     g.dma_start(mine, T.x[:, :]).then_inc(T.sem.loaded, 16)

@@ -14,13 +14,15 @@ def rank_program(g, core, T, topo):
         return
     me = topo.chip(core)
 
-    def way(c):
+    def turn(c):
         other = topo.chip(c)
         if topo.mates(me, other):
-            return 0
-        return 1 if topo.same_plane(me, other) else 2
+            way = 0
+        else:
+            way = 1 if topo.same_plane(me, other) else 2
+        return (-way, (other - me) % 8)
 
-    peers = sorted((c for c in T.cores if c != core), key=way, reverse=True)
+    peers = sorted((c for c in T.cores if c != core), key=turn)
     mine = T.land[:, W * rank:W * (rank + 1)]
 
     g.dma_start(mine, T.x[:, :]).then_inc(T.sem.loaded, 16)

from concourse.bass import DstId, RemoteDMATransfer

SCRATCH = {
    "land": ("sbuf", [128, 32], "bfloat16"),
}
SEMAPHORES = ["loaded", "arrived", "stored"]

W = 4


def rank_program(g, core, T, topo):
    rank = T.rank_of(core)
    if rank is None:
        return
    me = topo.chip(core)

    def turn(c):
        other = topo.chip(c)
        if topo.mates(me, other):
            way = 0
        else:
            way = 1 if topo.same_plane(me, other) else 2
        return (-way, (other - me) % 8)

    peers = sorted((c for c in T.cores if c != core), key=turn)
    mine = T.land[:, W * rank:W * (rank + 1)]

    g.dma_start(mine, T.x[:, :]).then_inc(T.sem.loaded, 16)
    g.wait_ge(T.sem.loaded, 16)

    ids = []
    for p in peers:
        rid, pid, _se = topo.addr(p)
        ids.append(DstId(rid=rid, pnc=pid))
    g.remote_dma_fused(
        [RemoteDMATransfer(dst_ids=ids, dma_engine_mask=0x00FF, remote_sem=T.sem.arrived,
                           srcs=[mine], dsts=[mine] * len(peers))],
        local_sem=T.sem.arrived)

    g.wait_ge(T.sem.arrived, 8 * len(peers) + 8)
    g.dma_start(T.y[:, :], T.land[:, :]).then_inc(T.sem.stored, 16)
    g.wait_ge(T.sem.stored, 16)
